import numpy as np
import ml_dtypes


def mxq(x, axis, fmt="e4m3"):
    dtype, down = {"e4m3": (ml_dtypes.float8_e4m3fn, 7), "e5m2": (ml_dtypes.float8_e5m2, 14)}[fmt]
    v = np.moveaxis(np.asarray(x, np.float32).astype(ml_dtypes.bfloat16).astype(np.float64), axis, -1)
    blocks = v.reshape(v.shape[:-1] + (-1, 32))
    amax = np.abs(blocks).max(-1, keepdims=True)
    byte = np.maximum(np.where(amax > 0, np.frexp(amax)[1] - 1 + 127, 0) - down, 1)
    scale = np.exp2(byte - 127.0)
    codes = (blocks / scale).astype(np.float32).astype(dtype).astype(np.float64)
    return np.moveaxis((codes * scale).reshape(v.shape), -1, axis)


WIDE = False


def mx_kscale(k):
    if not WIDE:
        return np.ones(k)
    levels = np.array([10, -10, 5, -5, 0])
    if k % 512:
        return np.exp2(np.random.permutation(np.resize(levels, k // 32))).repeat(32)
    a = np.empty((k // 512, 16))
    for p in range(k // 512):
        a[p, :8] = np.random.permutation(np.resize(levels, 8))
        for g in range(8):
            far = levels[np.abs(levels - a[p, g]) >= 10]
            a[p, g + 8] = far[np.random.randint(len(far))]
    return np.exp2(a.ravel()).repeat(32)


def f64(x):
    return np.asarray(x).astype(np.float64)


def striped(idx):
    return np.tile(idx.reshape(-1, 16).T, (8, 1)).astype(np.uint16)


def unstriped(offs):
    return offs[:16].T.reshape(-1).astype(np.int64)


E2M1 = np.array([0.0, 0.5, 1.0, 1.5, 2.0, 3.0, 4.0, 6.0, -0.0, -0.5, -1.0, -1.5, -2.0, -3.0, -4.0, -6.0])


def pack_weight(w, fmt):
    k, n = w.shape
    w = f64(np.asarray(w, np.float32).astype(ml_dtypes.bfloat16)).reshape(k // 32, 32, n)
    amax = np.abs(w).max(1)
    if fmt == "e4m3":
        byte = np.frexp(amax)[1] - 1 + 127 - 7
    else:
        mant, ex = np.frexp(amax / 6.0)
        byte = np.where(mant > 0.5, ex, ex - 1) + 127
    byte = np.clip(np.where(amax > 0, byte, 1), 1, 254)
    scaled = (w * np.exp2(127.0 - byte)[:, None, :]).reshape(k, n).astype(np.float32)
    by_word = np.ascontiguousarray(scaled.reshape(k // 512, 128, 4, n).transpose(0, 1, 3, 2))
    if fmt == "e4m3":
        words = by_word.astype(ml_dtypes.float8_e4m3fn).view(np.uint8)
    else:
        c = by_word.astype(ml_dtypes.float4_e2m1fn).view(np.uint8) & 0xF
        words = (c[..., 0::2] | (c[..., 1::2] << 4)).reshape(k // 512, 128, 2 * n)
    return np.ascontiguousarray(words), np.ascontiguousarray(byte.astype(np.uint8).reshape(k // 512, 16, n))


def unpack_weight(words, scales, fmt):
    g, _, n = scales.shape
    words = np.ascontiguousarray(words).reshape(g, 128, n, -1)
    if fmt == "e4m3":
        vals = words.view(ml_dtypes.float8_e4m3fn).astype(np.float64)
    else:
        nib = np.empty((g, 128, n, 4), np.uint8)
        nib[..., 0::2] = words & 0xF
        nib[..., 1::2] = words >> 4
        vals = E2M1[nib]
    vals = vals * np.repeat(np.exp2(scales.astype(np.float64) - 127.0), 8, axis=1)[..., None]
    return vals.transpose(0, 1, 3, 2).reshape(g * 512, n)


def silu(v):
    return v / (1.0 + np.exp(-np.maximum(v, -700.0)))


K, T, E, C, N = 1024, 1280, 8, 256, 384
K8 = 512


def by_expert(wq, xq):
    return np.concatenate([wq[e].T @ xq[:, e * C:(e + 1) * C] for e in range(E)], axis=1)


def setup_inputs():
    n = np.random.standard_normal
    s = mx_kscale(K)[:, None]
    w = n((E, K, N)) / np.sqrt(K) / s[None]
    w8 = [pack_weight(m[:K8], "e4m3") for m in w]
    w4 = [pack_weight(m[K8:], "e2m1") for m in w]
    idx = np.random.permutation(E * C)
    return {
        "xT": (n((K, T)) * s).astype(np.float32),
        "w8_words": np.stack([m[0] for m in w8]),
        "w8_scales": np.stack([m[1] for m in w8]),
        "w4_words": np.stack([m[0] for m in w4]),
        "w4_scales": np.stack([m[1] for m in w4]),
        "b": (0.3 * n((N, E))).astype(np.float32),
        "gate": np.tile(np.where(idx < T, np.random.uniform(0.2, 1.0, E * C), 0.0), (N, 1)).astype(np.float32),
        "offs": striped(idx),
    }


def reference(xT, w8_words, w8_scales, w4_words, w4_scales, b, gate, offs):
    idx = unstriped(offs)
    w = np.stack([np.concatenate([unpack_weight(w8_words[e], w8_scales[e], "e4m3"), unpack_weight(w4_words[e], w4_scales[e], "e2m1")]) for e in range(E)])
    xq = mxq(np.concatenate([f64(xT), np.zeros((K, E * C - T))], axis=1)[:, idx], 0, "e4m3")
    y = by_expert(w, xq)
    y = silu(y + np.repeat(f64(b), C, axis=1))
    out = np.zeros((N, E * C))
    out[:, idx] = f64(gate) * y
    return out[:, :T]

@@ -1,0 +1,171 @@
+from contextlib import ExitStack
+
+import concourse.mybir as mybir
+
+K, T, E, C, N = 1024, 1280, 8, 256, 384
+S = E * C
+FLOPS = 2 * K * N * S
+
+F32 = mybir.dt.float32
+BF16 = mybir.dt.bfloat16
+I32 = mybir.dt.int32
+U32 = mybir.dt.uint32
+U16 = mybir.dt.uint16
+U8 = mybir.dt.uint8
+FP8X4 = mybir.dt.float8_e4m3fn_x4
+FP4X4 = mybir.dt.float4_e2m1fn_x4
+ACT = mybir.ActivationFunctionType
+MULT = mybir.AluOpType.mult
+
+P = 128
+PACK = 4
+K_PASS = P * PACK
+BLOCKS = N // P
+HALF = S // 2
+EXPERTS_HALF = E // 2
+MOVE = 128
+ROW8 = 4
+ROW4 = 0
+CHUNKS = (
+    ((512, "vector"), (512, "vector"), (256, "vector")),
+    ((256, "scalar"), (512, "scalar"), (256, "scalar"), (256, "vector")),
+)
+
+
+def tile_moe_pad_lin_silu_kernel(
+    tc, xT, w8_words, w8_scales, w4_words, w4_scales, b, gate, offs, out
+):
+    nc = tc.nc
+    scale_row = (ROW8, ROW4)
+
+    with ExitStack() as ctx:
+        keep = ctx.enter_context(tc.tile_pool(name="keep", bufs=1))
+        psum = ctx.enter_context(tc.psum_pool(name="psum", bufs=8))
+
+        offsets = keep.tile([P, S // 16], U16, name="offsets")
+        token_words = [keep.tile([P, S], U32, name=f"token_words{a}", align_bytes=64) for a in range(2)]
+        token_scales = keep.tile([P, S], U8, name="token_scales", align_bytes=64)
+        w_scales = keep.tile([P, E, N], U8, name="w_scales", align_bytes=64)
+
+        nc.vector.memset(token_scales[:].bitcast(I32), 0)
+        nc.vector.memset(w_scales[:].bitcast(I32), 0)
+        for a in range(2):
+            nc.vector.memset(token_words[a][:, T:S].bitcast(I32), 0)
+
+        raw = {}
+        for a in range(2):
+            rows = xT[a * K_PASS : (a + 1) * K_PASS, :].rearrange("(p j) t -> p j t", j=PACK)
+            t0 = 0
+            for i, (width, engine) in enumerate(CHUNKS[a]):
+                raw[a, i] = keep.tile([P, PACK, width], F32, name=f"raw{a}_{i}")
+                nc.sync.dma_start(out=raw[a, i][:], in_=rows[:, :, t0 : t0 + width])
+                t0 = t0 + width
+            if a == 0:
+                nc.sync.dma_start(offsets[:], offs)
+
+        for scales, row in ((w8_scales, ROW8), (w4_scales, ROW4)):
+            for r in range(4):
+                nc.sync.dma_start(
+                    out=w_scales[row + r : P : 32, :, :].bitcast(I32),
+                    in_=scales[:, 0, r:16:4, :].rearrange("e q n -> q e n").bitcast(I32),
+                )
+
+        w8, w4, gates = [], [], []
+        bias = keep.tile([P, BLOCKS, E], F32, name="bias")
+        for h in range(2):
+            experts = slice(h * EXPERTS_HALF, (h + 1) * EXPERTS_HALF)
+            w8.append(keep.tile([P, EXPERTS_HALF, 4 * N], U8, name=f"w8_{h}", align_bytes=64))
+            nc.sync.dma_start(
+                out=w8[h][:].bitcast(I32),
+                in_=w8_words[experts, 0].rearrange("e p n r -> p e (n r)").bitcast(I32),
+            )
+            w4.append(keep.tile([P, EXPERTS_HALF, 2 * N], U8, name=f"w4_{h}", align_bytes=64))
+            nc.sync.dma_start(
+                out=w4[h][:].bitcast(I32),
+                in_=w4_words[experts, 0].rearrange("e p m -> p e m").bitcast(I32),
+            )
+            if h == 0:
+                nc.sync.dma_start(out=bias[:], in_=b.rearrange("(c p) e -> p c e", p=P))
+            gates.append(keep.tile([P, HALF], F32, name=f"gate{h}"))
+            nc.sync.dma_start(out=gates[h][:], in_=gate[0:P, h * HALF : (h + 1) * HALF])
+
+        def quantise(a):
+            t0 = 0
+            for i, (width, engine) in enumerate(CHUNKS[a]):
+                grouped = keep.tile([P, width, PACK], BF16, name=f"grouped{a}_{i}", align_bytes=64)
+                dst = grouped[:].rearrange("p (c i) j -> p c j i", i=4)
+                src = raw[a, i][:].rearrange("p j (c i) -> p c j i", i=4)
+                if engine == "vector":
+                    nc.vector.tensor_copy(out=dst, in_=src)
+                else:
+                    nc.scalar.activation(out=dst, in_=src, func=ACT.Copy)
+                nc.vector.quantize_mx(
+                    out=token_words[a][:, t0 : t0 + width].bitcast(FP8X4),
+                    scales=token_scales[scale_row[a] : P, t0 : t0 + width],
+                    in_=grouped[:].rearrange("p w j -> p (w j)"),
+                )
+                t0 = t0 + width
+
+        def half_list(h):
+            return offsets[:, h * HALF // 16 : (h + 1) * HALF // 16]
+
+        slot_words = {}
+        slot_scales = {}
+
+        def gather_words(a, h):
+            slot_words[a, h] = keep.tile([P, HALF], U32, name=f"slot_words{a}_{h}", align_bytes=64)
+            nc.vector.tensor_copy(slot_words[a, h][:], token_words[a][:].indirect(half_list(h)))
+
+        def gather_scales(h):
+            slot_scales[h] = keep.tile([P, HALF], U8, name=f"slot_scales{h}", align_bytes=64)
+            nc.vector.tensor_copy(slot_scales[h][:], token_scales[:].indirect(half_list(h)))
+
+        quantise(0)
+        for h in range(2):
+            gather_words(0, h)
+        quantise(1)
+        for h in range(2):
+            gather_words(1, h)
+            gather_scales(h)
+
+        y = {}
+        for h in range(2):
+            for c in range(BLOCKS):
+                y[h, c] = keep.tile([P, HALF], F32, name=f"y{h}_{c}")
+                for e in range(EXPERTS_HALF):
+                    acc = psum.tile([P, C], F32, name="acc")
+                    w_cols = slice(c * P, (c + 1) * P)
+                    for m in range(C // MOVE):
+                        slots = slice(e * C + m * MOVE, e * C + (m + 1) * MOVE)
+                        part = acc[:, m * MOVE : (m + 1) * MOVE]
+                        nc.tensor.matmul_mx(
+                            out=part,
+                            lhsT=w8[h][:, e, 4 * c * P : 4 * (c + 1) * P].bitcast(FP8X4),
+                            lhsT_scale=w_scales[ROW8:P, h * EXPERTS_HALF + e, w_cols],
+                            rhs=slot_words[0, h][:, slots].bitcast(FP8X4),
+                            rhs_scale=slot_scales[h][ROW8:P, slots],
+                            start=True,
+                            stop=False,
+                        )
+                        nc.tensor.matmul_mx(
+                            out=part,
+                            lhsT=w4[h][:, e, 2 * c * P : 2 * (c + 1) * P].bitcast(FP4X4),
+                            lhsT_scale=w_scales[ROW4:P, h * EXPERTS_HALF + e, w_cols],
+                            rhs=slot_words[1, h][:, slots].bitcast(FP8X4),
+                            rhs_scale=slot_scales[h][ROW4:P, slots],
+                            start=False,
+                            stop=True,
+                        )
+                    expert = h * EXPERTS_HALF + e
+                    nc.scalar.activation(
+                        out=y[h, c][:, e * C : (e + 1) * C],
+                        in_=acc[:],
+                        func=ACT.Silu,
+                        bias=bias[:, c, expert : expert + 1],
+                    )
+
+        windows = [keep.tile([P, S], F32, name=f"window{c}") for c in range(BLOCKS)]
+        for c, h in ((0, 0), (1, 0), (0, 1), (2, 0), (1, 1), (2, 1)):
+            nc.vector.tensor_tensor(windows[c][:].indirect(half_list(h)), y[h, c][:], gates[h][:], MULT)
+            if h == 1:
+                nc.sync.dma_start(out=out[c * P : (c + 1) * P, :], in_=windows[c][:, 0:T])

@@ -20,143 +20,154 @@ MULT = mybir.AluOpType.mult
 P = 128
 PACK = 4
 K_PASS = P * PACK
+PASSES = K // K_PASS
+QUADRANT = 32
+SCALE_ROWS = 16
+PER_COLUMN = 16
 BLOCKS = N // P
-HALF = S // 2
-EXPERTS_HALF = E // 2
-MOVE = 128
-ROW8 = 4
-ROW4 = 0
-CHUNKS = (
-    ((512, "vector"), (512, "vector"), (256, "vector")),
-    ((256, "scalar"), (512, "scalar"), (256, "scalar"), (256, "vector")),
+MOVING = 128
+LINE = 4
+W8_BYTES, W4_BYTES = 4, 2
+
+SCALE_ROW = (4, 0)
+
+LOADS = (
+    ((512, 256), (512, 256), (256, 160)),
+    ((128, 0), (256, 0), (256, 0), (256, 0), (256, 0), (128, 0)),
 )
+
+PARTS = (range(0, 2), range(2, E))
+
+WINDOW = 2 * C * len(PARTS[1])
 
 
 def tile_moe_pad_lin_silu_kernel(
     tc, xT, w8_words, w8_scales, w4_words, w4_scales, b, gate, offs, out
 ):
     nc = tc.nc
-    scale_row = (ROW8, ROW4)
 
     with ExitStack() as ctx:
         keep = ctx.enter_context(tc.tile_pool(name="keep", bufs=1))
         psum = ctx.enter_context(tc.psum_pool(name="psum", bufs=8))
 
-        offsets = keep.tile([P, S // 16], U16, name="offsets")
-        token_words = [keep.tile([P, S], U32, name=f"token_words{a}", align_bytes=64) for a in range(2)]
+        offsets = keep.tile([P, S // PER_COLUMN], U16, name="offsets")
+        token_words = [keep.tile([P, S], U32, name=f"token_words{a}", align_bytes=64) for a in range(PASSES)]
         token_scales = keep.tile([P, S], U8, name="token_scales", align_bytes=64)
         w_scales = keep.tile([P, E, N], U8, name="w_scales", align_bytes=64)
 
         nc.vector.memset(token_scales[:].bitcast(I32), 0)
         nc.vector.memset(w_scales[:].bitcast(I32), 0)
-        for a in range(2):
+        for a in range(PASSES):
             nc.vector.memset(token_words[a][:, T:S].bitcast(I32), 0)
 
         raw = {}
-        for a in range(2):
+        for a in range(PASSES):
             rows = xT[a * K_PASS : (a + 1) * K_PASS, :].rearrange("(p j) t -> p j t", j=PACK)
             t0 = 0
-            for i, (width, engine) in enumerate(CHUNKS[a]):
+            for i, (width, on_vector) in enumerate(LOADS[a]):
                 raw[a, i] = keep.tile([P, PACK, width], F32, name=f"raw{a}_{i}")
                 nc.sync.dma_start(out=raw[a, i][:], in_=rows[:, :, t0 : t0 + width])
                 t0 = t0 + width
             if a == 0:
                 nc.sync.dma_start(offsets[:], offs)
 
-        for scales, row in ((w8_scales, ROW8), (w4_scales, ROW4)):
+        for a, scales in enumerate((w8_scales, w4_scales)):
             for r in range(4):
                 nc.sync.dma_start(
-                    out=w_scales[row + r : P : 32, :, :].bitcast(I32),
-                    in_=scales[:, 0, r:16:4, :].rearrange("e q n -> q e n").bitcast(I32),
+                    out=w_scales[SCALE_ROW[a] + r : P : QUADRANT, :, :].bitcast(I32),
+                    in_=scales[:, 0, r:SCALE_ROWS:4, :].rearrange("e q n -> q e n").bitcast(I32),
                 )
 
         w8, w4, gates = [], [], []
         bias = keep.tile([P, BLOCKS, E], F32, name="bias")
-        for h in range(2):
-            experts = slice(h * EXPERTS_HALF, (h + 1) * EXPERTS_HALF)
-            w8.append(keep.tile([P, EXPERTS_HALF, 4 * N], U8, name=f"w8_{h}", align_bytes=64))
+        for h, experts in enumerate(PARTS):
+            first, end = experts.start, experts.stop
+            w8.append(keep.tile([P, len(experts), W8_BYTES * N], U8, name=f"w8_{h}", align_bytes=64))
             nc.sync.dma_start(
                 out=w8[h][:].bitcast(I32),
-                in_=w8_words[experts, 0].rearrange("e p n r -> p e (n r)").bitcast(I32),
+                in_=w8_words[first:end, 0].rearrange("e p n r -> p e (n r)").bitcast(I32),
             )
-            w4.append(keep.tile([P, EXPERTS_HALF, 2 * N], U8, name=f"w4_{h}", align_bytes=64))
+            w4.append(keep.tile([P, len(experts), W4_BYTES * N], U8, name=f"w4_{h}", align_bytes=64))
             nc.sync.dma_start(
                 out=w4[h][:].bitcast(I32),
-                in_=w4_words[experts, 0].rearrange("e p m -> p e m").bitcast(I32),
+                in_=w4_words[first:end, 0].rearrange("e p m -> p e m").bitcast(I32),
             )
             if h == 0:
                 nc.sync.dma_start(out=bias[:], in_=b.rearrange("(c p) e -> p c e", p=P))
-            gates.append(keep.tile([P, HALF], F32, name=f"gate{h}"))
-            nc.sync.dma_start(out=gates[h][:], in_=gate[0:P, h * HALF : (h + 1) * HALF])
+            gates.append(keep.tile([P, len(experts) * C], F32, name=f"gate{h}"))
+            nc.sync.dma_start(out=gates[h][:], in_=gate[0:P, first * C : end * C])
 
         def quantise(a):
             t0 = 0
-            for i, (width, engine) in enumerate(CHUNKS[a]):
+            for i, (width, on_vector) in enumerate(LOADS[a]):
                 grouped = keep.tile([P, width, PACK], BF16, name=f"grouped{a}_{i}", align_bytes=64)
-                dst = grouped[:].rearrange("p (c i) j -> p c j i", i=4)
-                src = raw[a, i][:].rearrange("p j (c i) -> p c j i", i=4)
-                if engine == "vector":
-                    nc.vector.tensor_copy(out=dst, in_=src)
-                else:
-                    nc.scalar.activation(out=dst, in_=src, func=ACT.Copy)
+                if on_vector > 0:
+                    nc.vector.tensor_copy(
+                        out=grouped[:, 0:on_vector, :].rearrange("p (g i) j -> p g j i", i=LINE),
+                        in_=raw[a, i][:, :, 0:on_vector].rearrange("p j (g i) -> p g j i", i=LINE),
+                    )
+                nc.scalar.activation(
+                    out=grouped[:, on_vector:width, :].rearrange("p (g i) j -> p g j i", i=LINE),
+                    in_=raw[a, i][:, :, on_vector:width].rearrange("p j (g i) -> p g j i", i=LINE),
+                    func=ACT.Copy,
+                )
                 nc.vector.quantize_mx(
                     out=token_words[a][:, t0 : t0 + width].bitcast(FP8X4),
-                    scales=token_scales[scale_row[a] : P, t0 : t0 + width],
-                    in_=grouped[:].rearrange("p w j -> p (w j)"),
+                    scales=token_scales[SCALE_ROW[a] : P, t0 : t0 + width],
+                    in_=grouped[:].rearrange("p t j -> p (t j)"),
                 )
                 t0 = t0 + width
 
-        def half_list(h):
-            return offsets[:, h * HALF // 16 : (h + 1) * HALF // 16]
+        def part_list(h):
+            return offsets[:, PARTS[h].start * C // PER_COLUMN : PARTS[h].stop * C // PER_COLUMN]
 
         slot_words = {}
         slot_scales = {}
 
         def gather_words(a, h):
-            slot_words[a, h] = keep.tile([P, HALF], U32, name=f"slot_words{a}_{h}", align_bytes=64)
-            nc.vector.tensor_copy(slot_words[a, h][:], token_words[a][:].indirect(half_list(h)))
+            slot_words[a, h] = keep.tile([P, len(PARTS[h]) * C], U32, name=f"slot_words{a}_{h}", align_bytes=64)
+            nc.vector.tensor_copy(slot_words[a, h][:], token_words[a][:].indirect(part_list(h)))
 
         def gather_scales(h):
-            slot_scales[h] = keep.tile([P, HALF], U8, name=f"slot_scales{h}", align_bytes=64)
-            nc.vector.tensor_copy(slot_scales[h][:], token_scales[:].indirect(half_list(h)))
+            slot_scales[h] = keep.tile([P, len(PARTS[h]) * C], U8, name=f"slot_scales{h}", align_bytes=64)
+            nc.vector.tensor_copy(slot_scales[h][:], token_scales[:].indirect(part_list(h)))
 
         quantise(0)
-        for h in range(2):
+        for h in range(len(PARTS)):
             gather_words(0, h)
         quantise(1)
-        for h in range(2):
+        for h in range(len(PARTS)):
             gather_words(1, h)
             gather_scales(h)
 
         y = {}
-        for h in range(2):
+        for h, experts in enumerate(PARTS):
             for c in range(BLOCKS):
-                y[h, c] = keep.tile([P, HALF], F32, name=f"y{h}_{c}")
-                for e in range(EXPERTS_HALF):
+                y[h, c] = keep.tile([P, len(experts) * C], F32, name=f"y{h}_{c}")
+                for e, expert in enumerate(experts):
                     acc = psum.tile([P, C], F32, name="acc")
                     w_cols = slice(c * P, (c + 1) * P)
-                    for m in range(C // MOVE):
-                        slots = slice(e * C + m * MOVE, e * C + (m + 1) * MOVE)
-                        part = acc[:, m * MOVE : (m + 1) * MOVE]
+                    for m in range(C // MOVING):
+                        slots = slice(e * C + m * MOVING, e * C + (m + 1) * MOVING)
+                        sums = acc[:, m * MOVING : (m + 1) * MOVING]
                         nc.tensor.matmul_mx(
-                            out=part,
-                            lhsT=w8[h][:, e, 4 * c * P : 4 * (c + 1) * P].bitcast(FP8X4),
-                            lhsT_scale=w_scales[ROW8:P, h * EXPERTS_HALF + e, w_cols],
+                            out=sums,
+                            lhsT=w8[h][:, e, W8_BYTES * c * P : W8_BYTES * (c + 1) * P].bitcast(FP8X4),
+                            lhsT_scale=w_scales[SCALE_ROW[0] : P, expert, w_cols],
                             rhs=slot_words[0, h][:, slots].bitcast(FP8X4),
-                            rhs_scale=slot_scales[h][ROW8:P, slots],
+                            rhs_scale=slot_scales[h][SCALE_ROW[0] : P, slots],
                             start=True,
                             stop=False,
                         )
                         nc.tensor.matmul_mx(
-                            out=part,
-                            lhsT=w4[h][:, e, 2 * c * P : 2 * (c + 1) * P].bitcast(FP4X4),
-                            lhsT_scale=w_scales[ROW4:P, h * EXPERTS_HALF + e, w_cols],
+                            out=sums,
+                            lhsT=w4[h][:, e, W4_BYTES * c * P : W4_BYTES * (c + 1) * P].bitcast(FP4X4),
+                            lhsT_scale=w_scales[SCALE_ROW[1] : P, expert, w_cols],
                             rhs=slot_words[1, h][:, slots].bitcast(FP8X4),
-                            rhs_scale=slot_scales[h][ROW4:P, slots],
+                            rhs_scale=slot_scales[h][SCALE_ROW[1] : P, slots],
                             start=False,
                             stop=True,
                         )
-                    expert = h * EXPERTS_HALF + e
                     nc.scalar.activation(
                         out=y[h, c][:, e * C : (e + 1) * C],
                         in_=acc[:],
@@ -164,8 +175,9 @@ def tile_moe_pad_lin_silu_kernel(
                         bias=bias[:, c, expert : expert + 1],
                     )
 
-        windows = [keep.tile([P, S], F32, name=f"window{c}") for c in range(BLOCKS)]
-        for c, h in ((0, 0), (1, 0), (0, 1), (2, 0), (1, 1), (2, 1)):
-            nc.vector.tensor_tensor(windows[c][:].indirect(half_list(h)), y[h, c][:], gates[h][:], MULT)
-            if h == 1:
-                nc.sync.dma_start(out=out[c * P : (c + 1) * P, :], in_=windows[c][:, 0:T])
+        windows = [keep.tile([P, WINDOW], F32, name=f"window{c}") for c in range(BLOCKS)]
+        for h in range(len(PARTS)):
+            for c in range(BLOCKS):
+                nc.vector.tensor_tensor(windows[c][:].indirect(part_list(h)), y[h, c][:], gates[h][:], MULT)
+                if h == len(PARTS) - 1:
+                    nc.sync.dma_start(out=out[c * P : (c + 1) * P, :], in_=windows[c][:, 0:T])

from contextlib import ExitStack

import concourse.mybir as mybir

K, T, E, C, N = 1024, 1280, 8, 256, 384
S = E * C
FLOPS = 2 * K * N * S

F32 = mybir.dt.float32
BF16 = mybir.dt.bfloat16
I32 = mybir.dt.int32
U32 = mybir.dt.uint32
U16 = mybir.dt.uint16
U8 = mybir.dt.uint8
FP8X4 = mybir.dt.float8_e4m3fn_x4
FP4X4 = mybir.dt.float4_e2m1fn_x4
ACT = mybir.ActivationFunctionType
MULT = mybir.AluOpType.mult

P = 128
PACK = 4
K_PASS = P * PACK
PASSES = K // K_PASS
QUADRANT = 32
SCALE_ROWS = 16
PER_COLUMN = 16
BLOCKS = N // P
MOVING = 128
LINE = 4
W8_BYTES, W4_BYTES = 4, 2

SCALE_ROW = (4, 0)

LOADS = (
    ((512, 256), (512, 256), (256, 160)),
    ((128, 0), (256, 0), (256, 0), (256, 0), (256, 0), (128, 0)),
)

PARTS = (range(0, 2), range(2, E))

WINDOW = 2 * C * len(PARTS[1])


def tile_moe_pad_lin_silu_kernel(
    tc, xT, w8_words, w8_scales, w4_words, w4_scales, b, gate, offs, out
):
    nc = tc.nc

    with ExitStack() as ctx:
        keep = ctx.enter_context(tc.tile_pool(name="keep", bufs=1))
        psum = ctx.enter_context(tc.psum_pool(name="psum", bufs=8))

        offsets = keep.tile([P, S // PER_COLUMN], U16, name="offsets")
        token_words = [keep.tile([P, S], U32, name=f"token_words{a}", align_bytes=64) for a in range(PASSES)]
        token_scales = keep.tile([P, S], U8, name="token_scales", align_bytes=64)
        w_scales = keep.tile([P, E, N], U8, name="w_scales", align_bytes=64)

        nc.vector.memset(token_scales[:].bitcast(I32), 0)
        nc.vector.memset(w_scales[:].bitcast(I32), 0)
        for a in range(PASSES):
            nc.vector.memset(token_words[a][:, T:S].bitcast(I32), 0)

        raw = {}
        for a in range(PASSES):
            rows = xT[a * K_PASS : (a + 1) * K_PASS, :].rearrange("(p j) t -> p j t", j=PACK)
            t0 = 0
            for i, (width, on_vector) in enumerate(LOADS[a]):
                raw[a, i] = keep.tile([P, PACK, width], F32, name=f"raw{a}_{i}")
                nc.sync.dma_start(out=raw[a, i][:], in_=rows[:, :, t0 : t0 + width])
                t0 = t0 + width
            if a == 0:
                nc.sync.dma_start(offsets[:], offs)

        for a, scales in enumerate((w8_scales, w4_scales)):
            for r in range(4):
                nc.sync.dma_start(
                    out=w_scales[SCALE_ROW[a] + r : P : QUADRANT, :, :].bitcast(I32),
                    in_=scales[:, 0, r:SCALE_ROWS:4, :].rearrange("e q n -> q e n").bitcast(I32),
                )

        w8, w4, gates = [], [], []
        bias = keep.tile([P, BLOCKS, E], F32, name="bias")
        for h, experts in enumerate(PARTS):
            first, end = experts.start, experts.stop
            w8.append(keep.tile([P, len(experts), W8_BYTES * N], U8, name=f"w8_{h}", align_bytes=64))
            nc.sync.dma_start(
                out=w8[h][:].bitcast(I32),
                in_=w8_words[first:end, 0].rearrange("e p n r -> p e (n r)").bitcast(I32),
            )
            w4.append(keep.tile([P, len(experts), W4_BYTES * N], U8, name=f"w4_{h}", align_bytes=64))
            nc.sync.dma_start(
                out=w4[h][:].bitcast(I32),
                in_=w4_words[first:end, 0].rearrange("e p m -> p e m").bitcast(I32),
            )
            if h == 0:
                nc.sync.dma_start(out=bias[:], in_=b.rearrange("(c p) e -> p c e", p=P))
            gates.append(keep.tile([P, len(experts) * C], F32, name=f"gate{h}"))
            nc.sync.dma_start(out=gates[h][:], in_=gate[0:P, first * C : end * C])

        def quantise(a):
            t0 = 0
            for i, (width, on_vector) in enumerate(LOADS[a]):
                grouped = keep.tile([P, width, PACK], BF16, name=f"grouped{a}_{i}", align_bytes=64)
                if on_vector > 0:
                    nc.vector.tensor_copy(
                        out=grouped[:, 0:on_vector, :].rearrange("p (g i) j -> p g j i", i=LINE),
                        in_=raw[a, i][:, :, 0:on_vector].rearrange("p j (g i) -> p g j i", i=LINE),
                    )
                nc.scalar.activation(
                    out=grouped[:, on_vector:width, :].rearrange("p (g i) j -> p g j i", i=LINE),
                    in_=raw[a, i][:, :, on_vector:width].rearrange("p j (g i) -> p g j i", i=LINE),
                    func=ACT.Copy,
                )
                nc.vector.quantize_mx(
                    out=token_words[a][:, t0 : t0 + width].bitcast(FP8X4),
                    scales=token_scales[SCALE_ROW[a] : P, t0 : t0 + width],
                    in_=grouped[:].rearrange("p t j -> p (t j)"),
                )
                t0 = t0 + width

        def part_list(h):
            return offsets[:, PARTS[h].start * C // PER_COLUMN : PARTS[h].stop * C // PER_COLUMN]

        slot_words = {}
        slot_scales = {}

        def gather_words(a, h):
            slot_words[a, h] = keep.tile([P, len(PARTS[h]) * C], U32, name=f"slot_words{a}_{h}", align_bytes=64)
            nc.vector.tensor_copy(slot_words[a, h][:], token_words[a][:].indirect(part_list(h)))

        def gather_scales(h):
            slot_scales[h] = keep.tile([P, len(PARTS[h]) * C], U8, name=f"slot_scales{h}", align_bytes=64)
            nc.vector.tensor_copy(slot_scales[h][:], token_scales[:].indirect(part_list(h)))

        quantise(0)
        for h in range(len(PARTS)):
            gather_words(0, h)
        quantise(1)
        for h in range(len(PARTS)):
            gather_words(1, h)
            gather_scales(h)

        y = {}
        for h, experts in enumerate(PARTS):
            for c in range(BLOCKS):
                y[h, c] = keep.tile([P, len(experts) * C], F32, name=f"y{h}_{c}")
                for e, expert in enumerate(experts):
                    acc = psum.tile([P, C], F32, name="acc")
                    w_cols = slice(c * P, (c + 1) * P)
                    for m in range(C // MOVING):
                        slots = slice(e * C + m * MOVING, e * C + (m + 1) * MOVING)
                        sums = acc[:, m * MOVING : (m + 1) * MOVING]
                        nc.tensor.matmul_mx(
                            out=sums,
                            lhsT=w8[h][:, e, W8_BYTES * c * P : W8_BYTES * (c + 1) * P].bitcast(FP8X4),
                            lhsT_scale=w_scales[SCALE_ROW[0] : P, expert, w_cols],
                            rhs=slot_words[0, h][:, slots].bitcast(FP8X4),
                            rhs_scale=slot_scales[h][SCALE_ROW[0] : P, slots],
                            start=True,
                            stop=False,
                        )
                        nc.tensor.matmul_mx(
                            out=sums,
                            lhsT=w4[h][:, e, W4_BYTES * c * P : W4_BYTES * (c + 1) * P].bitcast(FP4X4),
                            lhsT_scale=w_scales[SCALE_ROW[1] : P, expert, w_cols],
                            rhs=slot_words[1, h][:, slots].bitcast(FP8X4),
                            rhs_scale=slot_scales[h][SCALE_ROW[1] : P, slots],
                            start=False,
                            stop=True,
                        )
                    nc.scalar.activation(
                        out=y[h, c][:, e * C : (e + 1) * C],
                        in_=acc[:],
                        func=ACT.Silu,
                        bias=bias[:, c, expert : expert + 1],
                    )

        windows = [keep.tile([P, WINDOW], F32, name=f"window{c}") for c in range(BLOCKS)]
        for h in range(len(PARTS)):
            for c in range(BLOCKS):
                nc.vector.tensor_tensor(windows[c][:].indirect(part_list(h)), y[h, c][:], gates[h][:], MULT)
                if h == len(PARTS) - 1:
                    nc.sync.dma_start(out=out[c * P : (c + 1) * P, :], in_=windows[c][:, 0:T])
